import numpy as np
import ml_dtypes


def mxq(x, axis, fmt="e4m3"):
    dtype, down = {"e4m3": (ml_dtypes.float8_e4m3fn, 7), "e5m2": (ml_dtypes.float8_e5m2, 14)}[fmt]
    v = np.moveaxis(np.asarray(x, np.float32).astype(ml_dtypes.bfloat16).astype(np.float64), axis, -1)
    blocks = v.reshape(v.shape[:-1] + (-1, 32))
    amax = np.abs(blocks).max(-1, keepdims=True)
    byte = np.maximum(np.where(amax > 0, np.frexp(amax)[1] - 1 + 127, 0) - down, 1)
    scale = np.exp2(byte - 127.0)
    codes = (blocks / scale).astype(np.float32).astype(dtype).astype(np.float64)
    return np.moveaxis((codes * scale).reshape(v.shape), -1, axis)


WIDE = False


def mx_kscale(k):
    if not WIDE:
        return np.ones(k)
    levels = np.array([30, -30])
    if k % 512:
        return np.exp2(np.random.permutation(np.resize(levels, k // 32))).repeat(32)
    a = np.empty((k // 512, 16))
    for p in range(k // 512):
        a[p, :8] = np.random.permutation(np.resize(levels, 8))
        for g in range(8):
            far = levels[np.abs(levels - a[p, g]) >= 10]
            a[p, g + 8] = far[np.random.randint(len(far))]
    return np.exp2(a.ravel()).repeat(32)


def f64(x):
    return np.asarray(x).astype(np.float64)


def striped(idx):
    return np.tile(np.asarray(idx).reshape(-1, 16).T, (8, 1)).astype(np.uint16)


def unstriped(offs):
    return offs[:16].T.reshape(-1).astype(np.int64)


E2M1 = np.array([0.0, 0.5, 1.0, 1.5, 2.0, 3.0, 4.0, 6.0, -0.0, -0.5, -1.0, -1.5, -2.0, -3.0, -4.0, -6.0])


def pack_weight(w, fmt):
    k, n = w.shape
    w = f64(np.asarray(w, np.float32).astype(ml_dtypes.bfloat16)).reshape(k // 32, 32, n)
    amax = np.abs(w).max(1)
    if fmt in ("e4m3", "e5m2"):
        byte = np.frexp(amax)[1] - 1 + 127 - (7 if fmt == "e4m3" else 14)
    else:
        mant, ex = np.frexp(amax / 6.0)
        byte = np.where(mant > 0.5, ex, ex - 1) + 127
    byte = np.clip(np.where(amax > 0, byte, 1), 1, 254)
    scaled = (w * np.exp2(127.0 - byte)[:, None, :]).reshape(k, n).astype(np.float32)
    by_word = np.ascontiguousarray(scaled.reshape(k // 512, 128, 4, n).transpose(0, 1, 3, 2))
    if fmt in ("e4m3", "e5m2"):
        words = by_word.astype(ml_dtypes.float8_e4m3fn if fmt == "e4m3" else ml_dtypes.float8_e5m2).view(np.uint8)
    else:
        c = by_word.astype(ml_dtypes.float4_e2m1fn).view(np.uint8) & 0xF
        words = (c[..., 0::2] | (c[..., 1::2] << 4)).reshape(k // 512, 128, 2 * n)
    return np.ascontiguousarray(words), np.ascontiguousarray(byte.astype(np.uint8).reshape(k // 512, 16, n))


def unpack_weight(words, scales, fmt):
    g, _, n = scales.shape
    words = np.ascontiguousarray(words).reshape(g, 128, n, -1)
    if fmt in ("e4m3", "e5m2"):
        vals = words.view(ml_dtypes.float8_e4m3fn if fmt == "e4m3" else ml_dtypes.float8_e5m2).astype(np.float64)
    else:
        nib = np.empty((g, 128, n, 4), np.uint8)
        nib[..., 0::2] = words & 0xF
        nib[..., 1::2] = words >> 4
        vals = E2M1[nib]
    vals = vals * np.repeat(np.exp2(scales.astype(np.float64) - 127.0), 8, axis=1)[..., None]
    return vals.transpose(0, 1, 3, 2).reshape(g * 512, n)


def sigmoid(v):
    return 1.0 / (1.0 + np.exp(-v))


def sgn(shape):
    return np.random.uniform(0.5, 2.0, shape) * np.where(np.random.standard_normal(shape) < 0, -1.0, 1.0)


K, T, J, R, F, Z, N, C, O = 512, 1024, 256, 512, 512, 1024, 256, 512, 128


def setup_inputs():
    n = np.random.standard_normal
    idx = np.random.permutation(T)[:J]
    idx2 = np.random.permutation(Z)[:J]
    idx3 = np.random.permutation(C)[:J]
    idx4 = np.random.permutation(C)[:J]
    idx5 = np.random.permutation(J)[:O]
    idx6 = np.random.permutation(J)[:O]
    fk = mx_kscale(K)
    ff = mx_kscale(F)
    fr = mx_kscale(R)
    xtp = pack_weight(n((K, T)) / fk[:, None], "e2m1")
    xop = pack_weight(n((F, Z)) / ff[:, None], "e4m3")
    wp = pack_weight(n((K, R)) * 1 / np.sqrt(K) * fk[:, None] * fr, "e4m3")
    w2p = pack_weight(n((K, R)) * 1 / np.sqrt(K) * fk[:, None] * fr, "e5m2")
    w0p = pack_weight(n((F, R)) * 1 / np.sqrt(F) * ff[:, None] * fr, "e5m2")
    wbp = pack_weight(n((R, N)) * 1 / np.sqrt(R) / fr[:, None], "e2m1")
    wcp = pack_weight(n((R, N)) * 1 / np.sqrt(R) / fr[:, None], "e5m2")
    return {
        "xt_words": xtp[0],
        "xt_scales": xtp[1],
        "xo_words": xop[0],
        "xo_scales": xop[1],
        "w_words": wp[0],
        "w_scales": wp[1],
        "w2_words": w2p[0],
        "w2_scales": w2p[1],
        "w0_words": w0p[0],
        "w0_scales": w0p[1],
        "wb_words": wbp[0],
        "wb_scales": wbp[1],
        "wc_words": wcp[0],
        "wc_scales": wcp[1],
        "so": (np.random.uniform(0.5, 1.6, (N, 1))).astype(np.float32),
        "sp": (sgn((N, 1))).astype(np.float32),
        "bo": (np.random.uniform(-2.0, 2.0, (N, 1))).astype(np.float32),
        "offs": striped(idx),
        "offs2": striped(idx2),
        "offs3": striped(idx3),
        "offs4": striped(idx4),
        "offs5": striped(idx5),
        "offs6": striped(idx6),
    }


def reference(xt_words, xt_scales, xo_words, xo_scales, w_words, w_scales, w2_words, w2_scales, w0_words, w0_scales, wb_words, wb_scales, wc_words, wc_scales, so, sp, bo, offs, offs2, offs3, offs4, offs5, offs6):
    idx = unstriped(offs)
    idx2 = unstriped(offs2)
    idx3 = unstriped(offs3)
    idx4 = unstriped(offs4)
    idx5 = unstriped(offs5)
    idx6 = unstriped(offs6)
    xtu = unpack_weight(xt_words, xt_scales, "e2m1")
    xou = unpack_weight(xo_words, xo_scales, "e4m3")
    wu = unpack_weight(w_words, w_scales, "e4m3")
    w2u = unpack_weight(w2_words, w2_scales, "e5m2")
    w0u = unpack_weight(w0_words, w0_scales, "e5m2")
    wbu = unpack_weight(wb_words, wb_scales, "e2m1")
    wcu = unpack_weight(wc_words, wc_scales, "e5m2")
    xtidxg = xtu[:, idx]
    a = wu.T @ xtidxg
    xoidx2g = xou[:, idx2]
    b = w2u.T @ xtidxg + w0u.T @ xoidx2g
    hid = np.maximum(a, b)
    hidq = mxq(hid, 0, "e5m2")
    p = wbu.T @ hidq
    q = wcu.T @ hidq
    pw = np.zeros((N, C))
    pw[:, idx3] = p
    m0 = np.maximum(pw[:, idx4], q)
    y = m0[:, idx5] * f64(so) * sigmoid(m0[:, idx6] * f64(sp) + f64(bo))
    return y

@@ -1,0 +1,232 @@
+from contextlib import ExitStack
+
+import concourse.mybir as mybir
+from concourse.masks import make_identity
+
+K, T, J, R, F, Z, N, C, O = 512, 1024, 256, 512, 512, 1024, 256, 512, 128
+FLOPS = 2 * (K * R * J * 2 + F * R * J + R * N * J * 2)
+
+F32 = mybir.dt.float32
+BF16 = mybir.dt.bfloat16
+I32 = mybir.dt.int32
+U32 = mybir.dt.uint32
+U16 = mybir.dt.uint16
+U8 = mybir.dt.uint8
+E4M3 = mybir.dt.float8_e4m3fn_x4
+E5M2 = mybir.dt.float8_e5m2_x4
+E2M1 = mybir.dt.float4_e2m1fn_x4
+ALU = mybir.AluOpType
+ACT = mybir.ActivationFunctionType
+
+P = 128
+QUADS = 4
+
+
+def tile_list_outcomegatedchain_leaned_kernel(
+    tc, xt_words, xt_scales, xo_words, xo_scales, w_words, w_scales, w2_words, w2_scales,
+    w0_words, w0_scales, wb_words, wb_scales, wc_words, wc_scales, so, sp, bo,
+    offs, offs2, offs3, offs4, offs5, offs6, out,
+):
+    nc = tc.nc
+    with ExitStack() as ctx:
+        sb = ctx.enter_context(tc.tile_pool(name="sb", bufs=1))
+        ps = ctx.enter_context(tc.psum_pool(name="ps", bufs=1))
+
+        def tile(name, shape, dtype):
+            return sb.tile(shape, dtype, name=name, align_bytes=64)
+
+        def load_list(name, src):
+            dst = tile(name, list(src.shape), U16)
+            nc.sync.dma_start(dst[:], src)
+            return dst
+
+        def load_words(name, src, dtype):
+            rows = src[0] if src.ndim == 3 else src[0].rearrange("p n t -> p (n t)")
+            rows = rows.bitcast(I32)
+            words = rows.shape[1]
+            dst = tile(name, [P, words * (2 if dtype == U16 else 1)], dtype)
+            nc.sync.dma_start(dst[:].bitcast(I32), rows)
+            return dst
+
+        def zeroed_plane(name, width):
+            plane = tile(name, [P, width], U8)
+            nc.vector.memset(plane[:].bitcast(I32), 0)
+            return plane
+
+        def load_plane(queue, plane, src):
+            rows = src[0].bitcast(I32)
+            for q in range(QUADS):
+                queue.dma_start(plane[32 * q : 32 * q + 4, :].bitcast(I32), rows[4 * q : 4 * q + 4, :])
+
+        def load_folded(queues, dst, src):
+            rows = src[0].bitcast(I32).rearrange("(f q r) c -> q r f c", f=2, r=4)
+            for q in range(2):
+                queues[q].dma_start(dst[32 * q : 32 * q + 4], rows[q])
+
+        def zeroed_fold(name, parts, width):
+            fold = tile(name, [parts, 2, width // 4], I32)
+            nc.vector.memset(fold[:64], 0)
+            return fold
+
+        w_fold = zeroed_fold("w_fold", P, R)
+        xo_fold = zeroed_fold("xo_fold", 64, Z)
+        xt_plane = zeroed_plane("xt_plane", T)
+        w20_fold = zeroed_fold("w20_fold", P, 2 * R)
+        wb_plane = zeroed_plane("wb_plane", N)
+        wc_plane = zeroed_plane("wc_plane", N)
+        xo_plane = tile("xo_plane", [P, Z], U8)
+
+        xt_staged = tile("xt_staged", [4, QUADS, T // 4], I32)
+        idx = load_list("idx", offs)
+        nc.scalar.dma_start(xt_staged[:], xt_scales[0].bitcast(I32).rearrange("(q r) c -> r q c", r=4))
+        xt_sb = load_words("xt_sb", xt_words, U16)
+        load_folded((nc.scalar, nc.scalar), w_fold[:], w_scales)
+        w_sb = load_words("w_sb", w_words, U32)
+        w2_sb = load_words("w2_sb", w2_words, U32)
+        load_folded((nc.scalar, nc.scalar), xo_fold[:], xo_scales)
+        xo_sb = load_words("xo_sb", xo_words, U32)
+        idx2 = load_list("idx2", offs2)
+        load_folded((nc.scalar, nc.scalar), w20_fold[:, :, : R // 4], w2_scales)
+        w0_sb = load_words("w0_sb", w0_words, U32)
+        load_folded((nc.scalar, nc.sync), w20_fold[:, :, R // 4 :], w0_scales)
+        wb_sb = load_words("wb_sb", wb_words, U16)
+        load_plane(nc.sync, wb_plane, wb_scales)
+        idx3 = load_list("idx3", offs3)
+        wc_sb = load_words("wc_sb", wc_words, U32)
+        load_plane(nc.sync, wc_plane, wc_scales)
+        idx4 = load_list("idx4", offs4)
+        idx6 = load_list("idx6", offs6)
+        idx5 = load_list("idx5", offs5)
+        vecs = []
+        for name, src in (("sp_sb", sp), ("bo_sb", bo), ("so_sb", so)):
+            dst = tile(name, [P, 2], F32)
+            with nc.allow_non_contiguous_dma(reason="one value a partition and half"):
+                nc.sync.dma_start(dst[:], src.rearrange("(h p) o -> p (h o)", p=P))
+            vecs.append(dst)
+        sp_sb, bo_sb, so_sb = vecs
+
+        ident = tile("ident", [P, P], F32)
+        make_identity(nc, ident[:])
+        board = []
+        for h in range(2):
+            page = tile(f"board{h}", [P, C], F32)
+            nc.vector.memset(page[:], 0.0)
+            board.append(page)
+
+        xt_gs = tile("xt_gs", [P, J], U8)
+        xt_g = tile("xt_g", [P, J], U16)
+        xo_gs = tile("xo_gs", [P, J], U8)
+        xo_g = tile("xo_g", [P, J], U32)
+
+        def slots(s):
+            return slice(P * s, P * (s + 1))
+
+        def entries(s):
+            return slice(8 * s, 8 * (s + 1))
+
+        for q in range(QUADS):
+            nc.vector.tensor_copy(xt_plane[32 * q : 32 * q + 4, :].bitcast(I32), xt_staged[:, q, :])
+        nc.vector.tensor_copy(w_fold[64:, 0, :], w_fold[:64, 1, :])
+        w_plane = w_fold[:, 0, :].bitcast(U8)
+        for s in range(2):
+            nc.vector.tensor_copy(xt_gs[:, slots(s)], xt_plane[:].indirect(idx[:, entries(s)]))
+            nc.vector.tensor_copy(xt_g[:, slots(s)], xt_sb[:].indirect(idx[:, entries(s)]))
+
+        a_sb = []
+        for s in range(2):
+            a_ps = ps.tile([P, R], F32, name=f"a_ps{s}", tag=f"bank_a{s}")
+            nc.tensor.matmul_mx(
+                a_ps[:], lhsT=xt_g[:, slots(s)].bitcast(E2M1), lhsT_scale=xt_gs[:, slots(s)],
+                rhs=w_sb[:].bitcast(E4M3), rhs_scale=w_plane, start=True, stop=True,
+            )
+            dst = tile(f"a_sb{s}", [P, R], F32)
+            nc.scalar.copy(
+                dst[:].rearrange("j (u w e) -> j u w e", u=2, e=2),
+                a_ps[:].rearrange("j (w u e) -> j u w e", u=2, e=2),
+            )
+            a_sb.append(dst)
+
+        for f in range(2):
+            nc.vector.tensor_copy(xo_plane[64 * f : 64 * (f + 1), :].bitcast(I32), xo_fold[:, f, :])
+        nc.vector.tensor_copy(xo_gs[:], xo_plane[:].indirect(idx2[:]))
+        nc.vector.tensor_copy(w20_fold[64:, 0, :], w20_fold[:64, 1, :])
+        w20_plane = w20_fold[:, 0, :].bitcast(U8)
+        for s in range(2):
+            nc.vector.tensor_copy(xo_g[:, slots(s)], xo_sb[:].indirect(idx2[:, entries(s)]))
+
+        b_ps = [ps.tile([P, R], F32, name=f"b_ps{s}", tag=f"bank_b{s}") for s in range(2)]
+        for s in range(2):
+            nc.tensor.matmul_mx(
+                b_ps[s][:], lhsT=xt_g[:, slots(s)].bitcast(E2M1), lhsT_scale=xt_gs[:, slots(s)],
+                rhs=w2_sb[:].bitcast(E5M2), rhs_scale=w20_plane[:, :R], start=True, stop=False,
+            )
+            nc.tensor.matmul_mx(
+                b_ps[s][:], lhsT=xo_g[:, slots(s)].bitcast(E4M3), lhsT_scale=xo_gs[:, slots(s)],
+                rhs=w0_sb[:].bitcast(E5M2), rhs_scale=w20_plane[:, R:], start=False, stop=True,
+            )
+
+        hid_t = []
+        for s in range(2):
+            dst = tile(f"hid_t{s}", [P, R], BF16)
+            nc.vector.tensor_tensor(
+                dst[:].rearrange("j (u w e) -> j u w e", u=2, e=2),
+                b_ps[s][:].rearrange("j (w u e) -> j u w e", u=2, e=2),
+                a_sb[s][:].rearrange("j (u w e) -> j u w e", u=2, e=2),
+                ALU.max,
+            )
+            hid_t.append(dst)
+
+        hid_q = tile("hid_q", [P, J], U32)
+        hid_qs = tile("hid_qs", [P, J], U8)
+        for s in range(2):
+            turned = ps.tile([P, 2, P], F32, name=f"turned{s}", tag=f"bank_t{s}")
+            for u in range(2):
+                nc.tensor.transpose(turned[:, u, :], hid_t[s][:].bitcast(F32)[:, slots(u)], ident[:])
+            hid = tile(f"hid{s}", [P, 4 * P], BF16)
+            nc.scalar.copy(
+                hid[:].bitcast(F32).rearrange("p (j u) -> p j u", u=2),
+                turned[:].rearrange("p u j -> p j u"),
+            )
+            nc.vector.quantize_mx(hid_q[:, slots(s)].bitcast(E5M2), hid_qs[:, slots(s)], hid[:])
+        for s in range(2):
+            for h in range(2):
+                p_ps = ps.tile([P, P], F32, name=f"p_ps{s}{h}", tag=f"bank_{'ab'[s]}{h}")
+                nc.tensor.matmul_mx(
+                    p_ps[:], lhsT=wb_sb[:, slots(h)].bitcast(E2M1), lhsT_scale=wb_plane[:, slots(h)],
+                    rhs=hid_q[:, slots(s)].bitcast(E5M2), rhs_scale=hid_qs[:, slots(s)], start=True, stop=True,
+                )
+                p_sb = tile(f"p_sb{s}{h}", [P, P], F32)
+                places = board[h][:].indirect(idx3[:, entries(s)])
+                if h == 0:
+                    nc.vector.tensor_copy(p_sb[:], p_ps[:])
+                    nc.vector.tensor_copy(places, p_sb[:])
+                else:
+                    nc.scalar.copy(p_sb[:], p_ps[:])
+                    nc.scalar.activation(places, p_sb[:], ACT.Copy)
+
+        q_ps = []
+        for h in range(2):
+            bank = ps.tile([P, J], F32, name=f"q_ps{h}", tag=f"bank_q{h}")
+            nc.tensor.matmul_mx(
+                bank[:], lhsT=wc_sb[:, slots(h)].bitcast(E5M2), lhsT_scale=wc_plane[:, slots(h)],
+                rhs=hid_q[:].bitcast(E5M2), rhs_scale=hid_qs[:], start=True, stop=True,
+            )
+            q_ps.append(bank)
+
+        picked = [tile(f"picked{h}", [P, J], F32) for h in range(2)]
+        for h in range(2):
+            nc.vector.tensor_copy(picked[h][:, slots(0)], board[h][:].indirect(idx4[:, entries(0)]))
+            nc.scalar.activation(picked[h][:, slots(1)], board[h][:].indirect(idx4[:, entries(1)]), ACT.Copy)
+        for h in range(2):
+            m0 = tile(f"m0_{h}", [P, J], F32)
+            nc.vector.tensor_tensor(m0[:], q_ps[h][:], picked[h][:], ALU.max)
+            gate = tile(f"gate{h}", [P, O], F32)
+            val = tile(f"val{h}", [P, O], F32)
+            nc.scalar.activation(
+                gate[:], m0[:].indirect(idx6[:]), ACT.Sigmoid,
+                bias=bo_sb[:, h : h + 1], scale=sp_sb[:, h : h + 1],
+            )
+            nc.scalar.activation(val[:], m0[:].indirect(idx5[:]), ACT.Copy, scale=so_sb[:, h : h + 1])
+            res = tile(f"res{h}", [P, O], F32)
+            nc.vector.tensor_tensor(res[:], val[:], gate[:], ALU.mult)
+            nc.sync.dma_start(out[slots(h), :], res[:])

@@ -48,9 +48,9 @@ def tile_list_outcomegatedchain_leaned_kernel(
             nc.sync.dma_start(dst[:].bitcast(I32), rows)
             return dst
 
-        def zeroed_plane(name, width):
+        def zeroed_plane(engine, name, width):
             plane = tile(name, [P, width], U8)
-            nc.vector.memset(plane[:].bitcast(I32), 0)
+            engine.memset(plane[:].bitcast(I32), 0)
             return plane
 
         def load_plane(queue, plane, src):
@@ -58,37 +58,44 @@ def tile_list_outcomegatedchain_leaned_kernel(
             for q in range(QUADS):
                 queue.dma_start(plane[32 * q : 32 * q + 4, :].bitcast(I32), rows[4 * q : 4 * q + 4, :])
 
-        def load_folded(queues, dst, src):
+        def load_folded(queue, fold, base, src, q):
             rows = src[0].bitcast(I32).rearrange("(f q r) c -> q r f c", f=2, r=4)
-            for q in range(2):
-                queues[q].dma_start(dst[32 * q : 32 * q + 4], rows[q])
+            queue.dma_start(fold[base + 32 * q : base + 32 * q + 4], rows[q])
 
-        def zeroed_fold(name, parts, width):
-            fold = tile(name, [parts, 2, width // 4], I32)
-            nc.vector.memset(fold[:64], 0)
+        def zeroed_fold(engine, name, base, width):
+            fold = tile(name, [P, 2, width // 4], I32)
+            engine.memset(fold[base : base + 64], 0)
             return fold
 
-        w_fold = zeroed_fold("w_fold", P, R)
-        xo_fold = zeroed_fold("xo_fold", 64, Z)
-        xt_plane = zeroed_plane("xt_plane", T)
-        w20_fold = zeroed_fold("w20_fold", P, 2 * R)
-        wb_plane = zeroed_plane("wb_plane", N)
-        wc_plane = zeroed_plane("wc_plane", N)
+        xt_plane = zeroed_plane(nc.vector, "xt_plane", T)
+        ww2_plane = zeroed_plane(nc.vector, "ww2_plane", 2 * R)
+        xo_fold = zeroed_fold(nc.vector, "xo_fold", 64, Z)
+        w0_fold = zeroed_fold(nc.vector, "w0_fold", 0, R)
+        wb_plane = zeroed_plane(nc.gpsimd, "wb_plane", N)
+        wc_plane = zeroed_plane(nc.gpsimd, "wc_plane", N)
         xo_plane = tile("xo_plane", [P, Z], U8)
 
-        xt_staged = tile("xt_staged", [4, QUADS, T // 4], I32)
+        xt_staged = tile("xt_staged", [P, 2, T // 4], I32)
+        ww2_staged = tile("ww2_staged", [4, QUADS, 2 * R // 4], I32)
+        xt_rows = xt_scales[0].bitcast(I32).rearrange("(f q r) c -> f r q c", f=2, r=4)
         idx = load_list("idx", offs)
-        nc.scalar.dma_start(xt_staged[:], xt_scales[0].bitcast(I32).rearrange("(q r) c -> r q c", r=4))
+        nc.scalar.dma_start(xt_staged[0:4], xt_rows[0])
+        nc.scalar.dma_start(xt_staged[64:68], xt_rows[1])
+        for i, src in enumerate((w_scales, w2_scales)):
+            nc.sync.dma_start(
+                ww2_staged[:, :, i * R // 4 : (i + 1) * R // 4],
+                src[0].bitcast(I32).rearrange("(q r) c -> r q c", r=4),
+            )
         xt_sb = load_words("xt_sb", xt_words, U16)
-        load_folded((nc.scalar, nc.scalar), w_fold[:], w_scales)
         w_sb = load_words("w_sb", w_words, U32)
         w2_sb = load_words("w2_sb", w2_words, U32)
-        load_folded((nc.scalar, nc.scalar), xo_fold[:], xo_scales)
-        xo_sb = load_words("xo_sb", xo_words, U32)
         idx2 = load_list("idx2", offs2)
-        load_folded((nc.scalar, nc.scalar), w20_fold[:, :, : R // 4], w2_scales)
+        load_folded(nc.sync, xo_fold, 64, xo_scales, 0)
+        load_folded(nc.sync, xo_fold, 64, xo_scales, 1)
+        xo_sb = load_words("xo_sb", xo_words, U32)
+        load_folded(nc.sync, w0_fold, 0, w0_scales, 0)
+        load_folded(nc.sync, w0_fold, 0, w0_scales, 1)
         w0_sb = load_words("w0_sb", w0_words, U32)
-        load_folded((nc.scalar, nc.sync), w20_fold[:, :, R // 4 :], w0_scales)
         wb_sb = load_words("wb_sb", wb_words, U16)
         load_plane(nc.sync, wb_plane, wb_scales)
         idx3 = load_list("idx3", offs3)
@@ -110,9 +117,13 @@ def tile_list_outcomegatedchain_leaned_kernel(
         board = []
         for h in range(2):
             page = tile(f"board{h}", [P, C], F32)
-            nc.vector.memset(page[:], 0.0)
+            nc.gpsimd.memset(page[:], 0.0)
             board.append(page)
 
+        warm_in = tile("warm_in", [P, 1], F32)
+        warm_out = tile("warm_out", [P, 1], F32)
+        nc.vector.memset(warm_in[:], 0.0)
+        nc.scalar.activation(warm_out[:], warm_in[:], ACT.Sigmoid)
         xt_gs = tile("xt_gs", [P, J], U8)
         xt_g = tile("xt_g", [P, J], U16)
         xo_gs = tile("xo_gs", [P, J], U8)
@@ -125,55 +136,46 @@ def tile_list_outcomegatedchain_leaned_kernel(
             return slice(8 * s, 8 * (s + 1))
 
         for q in range(QUADS):
-            nc.vector.tensor_copy(xt_plane[32 * q : 32 * q + 4, :].bitcast(I32), xt_staged[:, q, :])
-        nc.vector.tensor_copy(w_fold[64:, 0, :], w_fold[:64, 1, :])
-        w_plane = w_fold[:, 0, :].bitcast(U8)
+            base = 64 * (q // 2)
+            nc.vector.tensor_copy(xt_plane[32 * q : 32 * q + 4, :].bitcast(I32), xt_staged[base : base + 4, q % 2, :])
+        for q in range(QUADS):
+            nc.vector.tensor_copy(ww2_plane[32 * q : 32 * q + 4, :].bitcast(I32), ww2_staged[:, q, :])
         for s in range(2):
             nc.vector.tensor_copy(xt_gs[:, slots(s)], xt_plane[:].indirect(idx[:, entries(s)]))
             nc.vector.tensor_copy(xt_g[:, slots(s)], xt_sb[:].indirect(idx[:, entries(s)]))
 
         a_sb = []
+        b_ps = [ps.tile([P, R], F32, name=f"b_ps{s}", tag=f"bank_b{s}") for s in range(2)]
         for s in range(2):
             a_ps = ps.tile([P, R], F32, name=f"a_ps{s}", tag=f"bank_a{s}")
             nc.tensor.matmul_mx(
                 a_ps[:], lhsT=xt_g[:, slots(s)].bitcast(E2M1), lhsT_scale=xt_gs[:, slots(s)],
-                rhs=w_sb[:].bitcast(E4M3), rhs_scale=w_plane, start=True, stop=True,
+                rhs=w_sb[:].bitcast(E4M3), rhs_scale=ww2_plane[:, :R], start=True, stop=True,
+            )
+            nc.tensor.matmul_mx(
+                b_ps[s][:], lhsT=xt_g[:, slots(s)].bitcast(E2M1), lhsT_scale=xt_gs[:, slots(s)],
+                rhs=w2_sb[:].bitcast(E5M2), rhs_scale=ww2_plane[:, R:], start=True, stop=False,
             )
             dst = tile(f"a_sb{s}", [P, R], F32)
-            nc.scalar.copy(
-                dst[:].rearrange("j (u w e) -> j u w e", u=2, e=2),
-                a_ps[:].rearrange("j (w u e) -> j u w e", u=2, e=2),
-            )
+            nc.scalar.copy(dst[:], a_ps[:])
             a_sb.append(dst)
 
         for f in range(2):
-            nc.vector.tensor_copy(xo_plane[64 * f : 64 * (f + 1), :].bitcast(I32), xo_fold[:, f, :])
+            nc.vector.tensor_copy(xo_plane[64 * f : 64 * (f + 1), :].bitcast(I32), xo_fold[64:, f, :])
         nc.vector.tensor_copy(xo_gs[:], xo_plane[:].indirect(idx2[:]))
-        nc.vector.tensor_copy(w20_fold[64:, 0, :], w20_fold[:64, 1, :])
-        w20_plane = w20_fold[:, 0, :].bitcast(U8)
+        nc.vector.tensor_copy(w0_fold[64:, 0, :], w0_fold[:64, 1, :])
+        w0_plane = w0_fold[:, 0, :].bitcast(U8)
         for s in range(2):
             nc.vector.tensor_copy(xo_g[:, slots(s)], xo_sb[:].indirect(idx2[:, entries(s)]))
-
-        b_ps = [ps.tile([P, R], F32, name=f"b_ps{s}", tag=f"bank_b{s}") for s in range(2)]
-        for s in range(2):
-            nc.tensor.matmul_mx(
-                b_ps[s][:], lhsT=xt_g[:, slots(s)].bitcast(E2M1), lhsT_scale=xt_gs[:, slots(s)],
-                rhs=w2_sb[:].bitcast(E5M2), rhs_scale=w20_plane[:, :R], start=True, stop=False,
-            )
             nc.tensor.matmul_mx(
                 b_ps[s][:], lhsT=xo_g[:, slots(s)].bitcast(E4M3), lhsT_scale=xo_gs[:, slots(s)],
-                rhs=w0_sb[:].bitcast(E5M2), rhs_scale=w20_plane[:, R:], start=False, stop=True,
+                rhs=w0_sb[:].bitcast(E5M2), rhs_scale=w0_plane, start=False, stop=True,
             )
 
         hid_t = []
         for s in range(2):
             dst = tile(f"hid_t{s}", [P, R], BF16)
-            nc.vector.tensor_tensor(
-                dst[:].rearrange("j (u w e) -> j u w e", u=2, e=2),
-                b_ps[s][:].rearrange("j (w u e) -> j u w e", u=2, e=2),
-                a_sb[s][:].rearrange("j (u w e) -> j u w e", u=2, e=2),
-                ALU.max,
-            )
+            nc.vector.tensor_tensor(dst[:], b_ps[s][:], a_sb[s][:], ALU.max)
             hid_t.append(dst)
 
         hid_q = tile("hid_q", [P, J], U32)
@@ -181,7 +183,7 @@ def tile_list_outcomegatedchain_leaned_kernel(
         for s in range(2):
             turned = ps.tile([P, 2, P], F32, name=f"turned{s}", tag=f"bank_t{s}")
             for u in range(2):
-                nc.tensor.transpose(turned[:, u, :], hid_t[s][:].bitcast(F32)[:, slots(u)], ident[:])
+                nc.tensor.transpose(turned[:, u, :], hid_t[s][:].bitcast(F32)[:, u : R // 2 : 2], ident[:])
             hid = tile(f"hid{s}", [P, 4 * P], BF16)
             nc.scalar.copy(
                 hid[:].bitcast(F32).rearrange("p (j u) -> p j u", u=2),
@@ -198,10 +200,10 @@ def tile_list_outcomegatedchain_leaned_kernel(
                 p_sb = tile(f"p_sb{s}{h}", [P, P], F32)
                 places = board[h][:].indirect(idx3[:, entries(s)])
                 if h == 0:
-                    nc.vector.tensor_copy(p_sb[:], p_ps[:])
+                    nc.scalar.copy(p_sb[:], p_ps[:])
                     nc.vector.tensor_copy(places, p_sb[:])
                 else:
-                    nc.scalar.copy(p_sb[:], p_ps[:])
+                    nc.vector.tensor_copy(p_sb[:], p_ps[:])
                     nc.scalar.activation(places, p_sb[:], ACT.Copy)
 
         q_ps = []

@@ -117,7 +117,7 @@ def tile_list_outcomegatedchain_leaned_kernel(
         board = []
         for h in range(2):
             page = tile(f"board{h}", [P, C], F32)
-            nc.gpsimd.memset(page[:], 0.0)
+            nc.vector.memset(page[:], 0.0)
             board.append(page)
 
         warm_in = tile("warm_in", [P, 1], F32)
@@ -200,10 +200,10 @@ def tile_list_outcomegatedchain_leaned_kernel(
                 p_sb = tile(f"p_sb{s}{h}", [P, P], F32)
                 places = board[h][:].indirect(idx3[:, entries(s)])
                 if h == 0:
-                    nc.scalar.copy(p_sb[:], p_ps[:])
+                    nc.vector.tensor_copy(p_sb[:], p_ps[:])
                     nc.vector.tensor_copy(places, p_sb[:])
                 else:
-                    nc.vector.tensor_copy(p_sb[:], p_ps[:])
+                    nc.scalar.copy(p_sb[:], p_ps[:])
                     nc.scalar.activation(places, p_sb[:], ACT.Copy)
 
         q_ps = []

from contextlib import ExitStack

import concourse.mybir as mybir
from concourse.masks import make_identity

K, T, J, R, F, Z, N, C, O = 512, 1024, 256, 512, 512, 1024, 256, 512, 128
FLOPS = 2 * (K * R * J * 2 + F * R * J + R * N * J * 2)

F32 = mybir.dt.float32
BF16 = mybir.dt.bfloat16
I32 = mybir.dt.int32
U32 = mybir.dt.uint32
U16 = mybir.dt.uint16
U8 = mybir.dt.uint8
E4M3 = mybir.dt.float8_e4m3fn_x4
E5M2 = mybir.dt.float8_e5m2_x4
E2M1 = mybir.dt.float4_e2m1fn_x4
ALU = mybir.AluOpType
ACT = mybir.ActivationFunctionType

P = 128
QUADS = 4


def tile_list_outcomegatedchain_leaned_kernel(
    tc, xt_words, xt_scales, xo_words, xo_scales, w_words, w_scales, w2_words, w2_scales,
    w0_words, w0_scales, wb_words, wb_scales, wc_words, wc_scales, so, sp, bo,
    offs, offs2, offs3, offs4, offs5, offs6, out,
):
    nc = tc.nc
    with ExitStack() as ctx:
        sb = ctx.enter_context(tc.tile_pool(name="sb", bufs=1))
        ps = ctx.enter_context(tc.psum_pool(name="ps", bufs=1))

        def tile(name, shape, dtype):
            return sb.tile(shape, dtype, name=name, align_bytes=64)

        def load_list(name, src):
            dst = tile(name, list(src.shape), U16)
            nc.sync.dma_start(dst[:], src)
            return dst

        def load_words(name, src, dtype):
            rows = src[0] if src.ndim == 3 else src[0].rearrange("p n t -> p (n t)")
            rows = rows.bitcast(I32)
            words = rows.shape[1]
            dst = tile(name, [P, words * (2 if dtype == U16 else 1)], dtype)
            nc.sync.dma_start(dst[:].bitcast(I32), rows)
            return dst

        def zeroed_plane(engine, name, width):
            plane = tile(name, [P, width], U8)
            engine.memset(plane[:].bitcast(I32), 0)
            return plane

        def load_plane(queue, plane, src):
            rows = src[0].bitcast(I32)
            for q in range(QUADS):
                queue.dma_start(plane[32 * q : 32 * q + 4, :].bitcast(I32), rows[4 * q : 4 * q + 4, :])

        def load_folded(queue, fold, base, src, q):
            rows = src[0].bitcast(I32).rearrange("(f q r) c -> q r f c", f=2, r=4)
            queue.dma_start(fold[base + 32 * q : base + 32 * q + 4], rows[q])

        def zeroed_fold(engine, name, base, width):
            fold = tile(name, [P, 2, width // 4], I32)
            engine.memset(fold[base : base + 64], 0)
            return fold

        xt_plane = zeroed_plane(nc.vector, "xt_plane", T)
        ww2_plane = zeroed_plane(nc.vector, "ww2_plane", 2 * R)
        xo_fold = zeroed_fold(nc.vector, "xo_fold", 64, Z)
        w0_fold = zeroed_fold(nc.vector, "w0_fold", 0, R)
        wb_plane = zeroed_plane(nc.gpsimd, "wb_plane", N)
        wc_plane = zeroed_plane(nc.gpsimd, "wc_plane", N)
        xo_plane = tile("xo_plane", [P, Z], U8)

        xt_staged = tile("xt_staged", [P, 2, T // 4], I32)
        ww2_staged = tile("ww2_staged", [4, QUADS, 2 * R // 4], I32)
        xt_rows = xt_scales[0].bitcast(I32).rearrange("(f q r) c -> f r q c", f=2, r=4)
        idx = load_list("idx", offs)
        nc.scalar.dma_start(xt_staged[0:4], xt_rows[0])
        nc.scalar.dma_start(xt_staged[64:68], xt_rows[1])
        for i, src in enumerate((w_scales, w2_scales)):
            nc.sync.dma_start(
                ww2_staged[:, :, i * R // 4 : (i + 1) * R // 4],
                src[0].bitcast(I32).rearrange("(q r) c -> r q c", r=4),
            )
        xt_sb = load_words("xt_sb", xt_words, U16)
        w_sb = load_words("w_sb", w_words, U32)
        w2_sb = load_words("w2_sb", w2_words, U32)
        idx2 = load_list("idx2", offs2)
        load_folded(nc.sync, xo_fold, 64, xo_scales, 0)
        load_folded(nc.sync, xo_fold, 64, xo_scales, 1)
        xo_sb = load_words("xo_sb", xo_words, U32)
        load_folded(nc.sync, w0_fold, 0, w0_scales, 0)
        load_folded(nc.sync, w0_fold, 0, w0_scales, 1)
        w0_sb = load_words("w0_sb", w0_words, U32)
        wb_sb = load_words("wb_sb", wb_words, U16)
        load_plane(nc.sync, wb_plane, wb_scales)
        idx3 = load_list("idx3", offs3)
        wc_sb = load_words("wc_sb", wc_words, U32)
        load_plane(nc.sync, wc_plane, wc_scales)
        idx4 = load_list("idx4", offs4)
        idx6 = load_list("idx6", offs6)
        idx5 = load_list("idx5", offs5)
        vecs = []
        for name, src in (("sp_sb", sp), ("bo_sb", bo), ("so_sb", so)):
            dst = tile(name, [P, 2], F32)
            with nc.allow_non_contiguous_dma(reason="one value a partition and half"):
                nc.sync.dma_start(dst[:], src.rearrange("(h p) o -> p (h o)", p=P))
            vecs.append(dst)
        sp_sb, bo_sb, so_sb = vecs

        ident = tile("ident", [P, P], F32)
        make_identity(nc, ident[:])
        board = []
        for h in range(2):
            page = tile(f"board{h}", [P, C], F32)
            nc.vector.memset(page[:], 0.0)
            board.append(page)

        warm_in = tile("warm_in", [P, 1], F32)
        warm_out = tile("warm_out", [P, 1], F32)
        nc.vector.memset(warm_in[:], 0.0)
        nc.scalar.activation(warm_out[:], warm_in[:], ACT.Sigmoid)
        xt_gs = tile("xt_gs", [P, J], U8)
        xt_g = tile("xt_g", [P, J], U16)
        xo_gs = tile("xo_gs", [P, J], U8)
        xo_g = tile("xo_g", [P, J], U32)

        def slots(s):
            return slice(P * s, P * (s + 1))

        def entries(s):
            return slice(8 * s, 8 * (s + 1))

        for q in range(QUADS):
            base = 64 * (q // 2)
            nc.vector.tensor_copy(xt_plane[32 * q : 32 * q + 4, :].bitcast(I32), xt_staged[base : base + 4, q % 2, :])
        for q in range(QUADS):
            nc.vector.tensor_copy(ww2_plane[32 * q : 32 * q + 4, :].bitcast(I32), ww2_staged[:, q, :])
        for s in range(2):
            nc.vector.tensor_copy(xt_gs[:, slots(s)], xt_plane[:].indirect(idx[:, entries(s)]))
            nc.vector.tensor_copy(xt_g[:, slots(s)], xt_sb[:].indirect(idx[:, entries(s)]))

        a_sb = []
        b_ps = [ps.tile([P, R], F32, name=f"b_ps{s}", tag=f"bank_b{s}") for s in range(2)]
        for s in range(2):
            a_ps = ps.tile([P, R], F32, name=f"a_ps{s}", tag=f"bank_a{s}")
            nc.tensor.matmul_mx(
                a_ps[:], lhsT=xt_g[:, slots(s)].bitcast(E2M1), lhsT_scale=xt_gs[:, slots(s)],
                rhs=w_sb[:].bitcast(E4M3), rhs_scale=ww2_plane[:, :R], start=True, stop=True,
            )
            nc.tensor.matmul_mx(
                b_ps[s][:], lhsT=xt_g[:, slots(s)].bitcast(E2M1), lhsT_scale=xt_gs[:, slots(s)],
                rhs=w2_sb[:].bitcast(E5M2), rhs_scale=ww2_plane[:, R:], start=True, stop=False,
            )
            dst = tile(f"a_sb{s}", [P, R], F32)
            nc.scalar.copy(dst[:], a_ps[:])
            a_sb.append(dst)

        for f in range(2):
            nc.vector.tensor_copy(xo_plane[64 * f : 64 * (f + 1), :].bitcast(I32), xo_fold[64:, f, :])
        nc.vector.tensor_copy(xo_gs[:], xo_plane[:].indirect(idx2[:]))
        nc.vector.tensor_copy(w0_fold[64:, 0, :], w0_fold[:64, 1, :])
        w0_plane = w0_fold[:, 0, :].bitcast(U8)
        for s in range(2):
            nc.vector.tensor_copy(xo_g[:, slots(s)], xo_sb[:].indirect(idx2[:, entries(s)]))
            nc.tensor.matmul_mx(
                b_ps[s][:], lhsT=xo_g[:, slots(s)].bitcast(E4M3), lhsT_scale=xo_gs[:, slots(s)],
                rhs=w0_sb[:].bitcast(E5M2), rhs_scale=w0_plane, start=False, stop=True,
            )

        hid_t = []
        for s in range(2):
            dst = tile(f"hid_t{s}", [P, R], BF16)
            nc.vector.tensor_tensor(dst[:], b_ps[s][:], a_sb[s][:], ALU.max)
            hid_t.append(dst)

        hid_q = tile("hid_q", [P, J], U32)
        hid_qs = tile("hid_qs", [P, J], U8)
        for s in range(2):
            turned = ps.tile([P, 2, P], F32, name=f"turned{s}", tag=f"bank_t{s}")
            for u in range(2):
                nc.tensor.transpose(turned[:, u, :], hid_t[s][:].bitcast(F32)[:, u : R // 2 : 2], ident[:])
            hid = tile(f"hid{s}", [P, 4 * P], BF16)
            nc.scalar.copy(
                hid[:].bitcast(F32).rearrange("p (j u) -> p j u", u=2),
                turned[:].rearrange("p u j -> p j u"),
            )
            nc.vector.quantize_mx(hid_q[:, slots(s)].bitcast(E5M2), hid_qs[:, slots(s)], hid[:])
        for s in range(2):
            for h in range(2):
                p_ps = ps.tile([P, P], F32, name=f"p_ps{s}{h}", tag=f"bank_{'ab'[s]}{h}")
                nc.tensor.matmul_mx(
                    p_ps[:], lhsT=wb_sb[:, slots(h)].bitcast(E2M1), lhsT_scale=wb_plane[:, slots(h)],
                    rhs=hid_q[:, slots(s)].bitcast(E5M2), rhs_scale=hid_qs[:, slots(s)], start=True, stop=True,
                )
                p_sb = tile(f"p_sb{s}{h}", [P, P], F32)
                places = board[h][:].indirect(idx3[:, entries(s)])
                if h == 0:
                    nc.vector.tensor_copy(p_sb[:], p_ps[:])
                    nc.vector.tensor_copy(places, p_sb[:])
                else:
                    nc.scalar.copy(p_sb[:], p_ps[:])
                    nc.scalar.activation(places, p_sb[:], ACT.Copy)

        q_ps = []
        for h in range(2):
            bank = ps.tile([P, J], F32, name=f"q_ps{h}", tag=f"bank_q{h}")
            nc.tensor.matmul_mx(
                bank[:], lhsT=wc_sb[:, slots(h)].bitcast(E5M2), lhsT_scale=wc_plane[:, slots(h)],
                rhs=hid_q[:].bitcast(E5M2), rhs_scale=hid_qs[:], start=True, stop=True,
            )
            q_ps.append(bank)

        picked = [tile(f"picked{h}", [P, J], F32) for h in range(2)]
        for h in range(2):
            nc.vector.tensor_copy(picked[h][:, slots(0)], board[h][:].indirect(idx4[:, entries(0)]))
            nc.scalar.activation(picked[h][:, slots(1)], board[h][:].indirect(idx4[:, entries(1)]), ACT.Copy)
        for h in range(2):
            m0 = tile(f"m0_{h}", [P, J], F32)
            nc.vector.tensor_tensor(m0[:], q_ps[h][:], picked[h][:], ALU.max)
            gate = tile(f"gate{h}", [P, O], F32)
            val = tile(f"val{h}", [P, O], F32)
            nc.scalar.activation(
                gate[:], m0[:].indirect(idx6[:]), ACT.Sigmoid,
                bias=bo_sb[:, h : h + 1], scale=sp_sb[:, h : h + 1],
            )
            nc.scalar.activation(val[:], m0[:].indirect(idx5[:]), ACT.Copy, scale=so_sb[:, h : h + 1])
            res = tile(f"res{h}", [P, O], F32)
            nc.vector.tensor_tensor(res[:], val[:], gate[:], ALU.mult)
            nc.sync.dma_start(out[slots(h), :], res[:])
